import numpy as np
import ml_dtypes


def mxq(x, axis, fmt="e4m3"):
    dtype, down = {"e4m3": (ml_dtypes.float8_e4m3fn, 7), "e5m2": (ml_dtypes.float8_e5m2, 14)}[fmt]
    v = np.moveaxis(np.asarray(x, np.float32).astype(ml_dtypes.bfloat16).astype(np.float64), axis, -1)
    blocks = v.reshape(v.shape[:-1] + (-1, 32))
    amax = np.abs(blocks).max(-1, keepdims=True)
    byte = np.maximum(np.where(amax > 0, np.frexp(amax)[1] - 1 + 127, 0) - down, 1)
    scale = np.exp2(byte - 127.0)
    codes = (blocks / scale).astype(np.float32).astype(dtype).astype(np.float64)
    return np.moveaxis((codes * scale).reshape(v.shape), -1, axis)


WIDE = False


def mx_kscale(k):
    if not WIDE:
        return np.ones(k)
    levels = np.array([10, -10, 5, -5, 0])
    if k % 512:
        return np.exp2(np.random.permutation(np.resize(levels, k // 32))).repeat(32)
    a = np.empty((k // 512, 16))
    for p in range(k // 512):
        a[p, :8] = np.random.permutation(np.resize(levels, 8))
        for g in range(8):
            far = levels[np.abs(levels - a[p, g]) >= 10]
            a[p, g + 8] = far[np.random.randint(len(far))]
    return np.exp2(a.ravel()).repeat(32)


def f64(x):
    return np.asarray(x).astype(np.float64)


def striped(idx):
    return np.tile(idx.reshape(-1, 16).T, (8, 1)).astype(np.uint16)


def unstriped(offs):
    return offs[:16].T.reshape(-1).astype(np.int64)


E2M1 = np.array([0.0, 0.5, 1.0, 1.5, 2.0, 3.0, 4.0, 6.0, -0.0, -0.5, -1.0, -1.5, -2.0, -3.0, -4.0, -6.0])


def pack_weight(w, fmt):
    k, n = w.shape
    w = f64(np.asarray(w, np.float32).astype(ml_dtypes.bfloat16)).reshape(k // 32, 32, n)
    amax = np.abs(w).max(1)
    if fmt == "e4m3":
        byte = np.frexp(amax)[1] - 1 + 127 - 7
    else:
        mant, ex = np.frexp(amax / 6.0)
        byte = np.where(mant > 0.5, ex, ex - 1) + 127
    byte = np.clip(np.where(amax > 0, byte, 1), 1, 254)
    scaled = (w * np.exp2(127.0 - byte)[:, None, :]).reshape(k, n).astype(np.float32)
    by_word = np.ascontiguousarray(scaled.reshape(k // 512, 128, 4, n).transpose(0, 1, 3, 2))
    if fmt == "e4m3":
        words = by_word.astype(ml_dtypes.float8_e4m3fn).view(np.uint8)
    else:
        c = by_word.astype(ml_dtypes.float4_e2m1fn).view(np.uint8) & 0xF
        words = (c[..., 0::2] | (c[..., 1::2] << 4)).reshape(k // 512, 128, 2 * n)
    return np.ascontiguousarray(words), np.ascontiguousarray(byte.astype(np.uint8).reshape(k // 512, 16, n))


def unpack_weight(words, scales, fmt):
    g, _, n = scales.shape
    words = np.ascontiguousarray(words).reshape(g, 128, n, -1)
    if fmt == "e4m3":
        vals = words.view(ml_dtypes.float8_e4m3fn).astype(np.float64)
    else:
        nib = np.empty((g, 128, n, 4), np.uint8)
        nib[..., 0::2] = words & 0xF
        nib[..., 1::2] = words >> 4
        vals = E2M1[nib]
    vals = vals * np.repeat(np.exp2(scales.astype(np.float64) - 127.0), 8, axis=1)[..., None]
    return vals.transpose(0, 1, 3, 2).reshape(g * 512, n)


def gelu(v):
    return 0.5 * v * (1.0 + np.tanh(np.sqrt(2.0 / np.pi) * (v + 0.044715 * v**3)))


def bf(x):
    return np.asarray(x, np.float32).astype(ml_dtypes.bfloat16)


def planes(Y):
    n, m = Y.shape
    b = f64(bf(Y)).reshape(n // 32, 32, m)
    amax = np.abs(b).max(1)
    byte = np.clip(np.where(amax > 0, np.frexp(amax)[1] - 1 + 127 - 7, 1), 1, 254)
    codes = (b * np.exp2(127.0 - byte)[:, None, :]).reshape(n, m).astype(np.float32).astype(ml_dtypes.float8_e4m3fn).view(np.uint8)
    words = codes.reshape(n // 512, 128, 4, m).transpose(0, 1, 3, 2)
    return np.ascontiguousarray(words), np.ascontiguousarray(byte.astype(np.uint8).reshape(n // 512, 16, m))


K, H, N, T, S, T2, P = 1536, 1024, 256, 2048, 1024, 2048, 1024

def setup_inputs():
    n = np.random.standard_normal
    s = mx_kscale(K)[:, None]
    u = mx_kscale(H)[:, None]
    d = {}
    d["tab_words"], d["tab_scales"] = pack_weight(n((K, T)) * s, "e4m3")
    d["offs"] = striped(np.random.permutation(T)[:S])
    d["offs2"] = striped(np.random.permutation(T2)[:S])
    d["offs3"] = striped(np.random.permutation(T2)[:P])
    d["w1"] = (1.5 * n((K, H)) / K ** 0.5 / s).astype(np.float32)
    d["gain"] = (1.6 * np.exp(0.3 * n(H)) * u[:, 0]).astype(np.float32)
    d["wgs"] = np.exp(0.3 * n((128, S))).astype(np.float32)
    d["page0"] = (0.9 * n((H, T2)) * u).astype(np.float32)
    d["bias"] = (0.6 * n(H) * u[:, 0]).astype(np.float32)
    d["w4_words"], d["w4_scales"] = pack_weight(n((H, N)) / H ** 0.5 / u, "e2m1")
    d["w3"] = (n((H, N)) / H ** 0.5 / u).astype(np.float32)
    return d

def reference(tab_words, tab_scales, offs, offs2, offs3, w1, gain, wgs, page0, bias, w4_words, w4_scales, w3):
    v = unpack_weight(tab_words, tab_scales, "e4m3")[:, unstriped(offs)]
    z = mxq(f64(w1), 0, "e4m3").T @ v
    h = f64(gain)[:, None] * np.exp(-np.abs(z))
    page = f64(page0).copy()
    page[:, unstriped(offs2)] = np.tile(f64(wgs), (H // 128, 1)) * h
    x = page[:, unstriped(offs3)] + f64(bias)[:, None]
    xq = mxq(x, 0, "e4m3")
    w4 = unpack_weight(w4_words, w4_scales, "e2m1")
    y1 = w4.T @ xq
    y2 = mxq(f64(w3), 0, "e4m3").T @ xq
    y = np.maximum(y1, y2)
    words, scales = planes(page)
    return y, page, words, scales

@@ -1,0 +1,396 @@
+from contextlib import ExitStack
+
+import concourse.mybir as mybir
+
+K, H, N, T, S, T2, PX = 1536, 1024, 256, 2048, 1024, 2048, 1024
+FLOPS = 2 * K * H * S + 2 * 2 * H * N * PX
+
+F32 = mybir.dt.float32
+BF16 = mybir.dt.bfloat16
+I32 = mybir.dt.int32
+U32 = mybir.dt.uint32
+U16 = mybir.dt.uint16
+U8 = mybir.dt.uint8
+FP8X4 = mybir.dt.float8_e4m3fn_x4
+FP4X4 = mybir.dt.float4_e2m1fn_x4
+ALU = mybir.AluOpType
+ACT = mybir.ActivationFunctionType
+
+P = 128
+PACK = 4
+KP = P * PACK
+PASSES = K // KP
+GROUPS = H // KP
+SLICES = GROUPS * PACK
+HALF = 512
+LIST_HALF = HALF // 16
+CHUNKS = T2 // HALF
+NCH = N // P
+
+
+def tile_list_herbal_alert_scores_kernel(
+    tc, tab_words, tab_scales, offs, offs2, offs3, w1, gain, wgs, page0, bias, w4_words, w4_scales, w3,
+    out_0, out_1, out_2, out_3,
+):
+    nc = tc.nc
+    with ExitStack() as ctx:
+        lists = ctx.enter_context(tc.tile_pool(name="lists", bufs=1))
+        sb = ctx.enter_context(tc.tile_pool(name="sb", bufs=1))
+        ps = ctx.enter_context(tc.psum_pool(name="ps", bufs=1))
+
+        def tile(name, shape, dtype, tag=None):
+            return sb.tile(shape, dtype, name=name, tag=tag or name, align_bytes=64)
+
+        def half(i):
+            return slice(i * HALF, (i + 1) * HALF)
+
+        def list_half(i):
+            return slice(i * LIST_HALF, (i + 1) * LIST_HALF)
+
+        idx = lists.tile([P, S // 16], U16, name="idx")
+        idx2 = lists.tile([P, S // 16], U16, name="idx2")
+        idx3 = lists.tile([P, PX // 16], U16, name="idx3")
+        banks = [ps.tile([P, HALF], F32, name="bank%d" % b) for b in range(8)]
+
+        gain_sb = tile("gain_sb", [P, GROUPS, PACK], F32)
+        bias_sb = tile("bias_sb", [P, GROUPS, PACK], F32)
+        tabw = [tile("tabw%d" % a, [P, T], U32) for a in range(PASSES)]
+        tabs = tile("tabs", [P, T], U8)
+        vw = [tile("vw%d" % a, [P, S], U32) for a in range(PASSES)]
+        vs = tile("vs", [P, S], U8)
+        raw = [tile("raw%d" % a, [P, PACK * HALF], F32) for a in range(PASSES)]
+        stage = [tile("stage%d" % i, [P, PACK * HALF], BF16) for i in range(7)]
+        w1c = {(0, a): tile("w1c0%d" % a, [P, KP], U32) for a in range(PASSES)}
+        w1s = [[tile("w1s%d%d" % (g, a), [P, KP], U8) for a in range(PASSES)] for g in range(GROUPS)]
+        wgs_sb = [tile("wgs%d" % t, [P, S], F32) for t in range(PACK)]
+        page = {s: tile("page%d" % s, [P, T2], F32) for s in range(SLICES)}
+        w4c = tile("w4c", [P, GROUPS, 2 * N], U8)
+        w4s = tile("w4s", [P, GROUPS, N], U8)
+        w3s = tile("w3s", [P, GROUPS * N], U8)
+        hbuf = [tile("h%d" % i, [P, S], F32) for i in range(4)]
+        late = {}
+        xg = [tile("xg%d" % i, [P, PX], F32) for i in range(2)]
+        xc = {}
+        xs = [tile("xs%d" % g, [P, PX], U8) for g in range(GROUPS)]
+        planes_s = {1: tile("planes_s1", [P, T2], U8)}
+        quad = {c: tile("quad%d" % c, [P, PACK, HALF], F32) for c in range(3)}
+        planes_c = {}
+        xil = {}
+
+        page0_v = page0.rearrange("(g p t) m -> g t p m", g=GROUPS, t=PACK)
+        out1_v = out_1.rearrange("(g p t) m -> g t p m", g=GROUPS, t=PACK)
+        wgs_v = wgs.rearrange("(q t) j -> t q j", t=PACK)
+
+        def load_table(a):
+            nc.sync.dma_start(tabw[a][:].bitcast(I32), tab_words[a].rearrange("p t i -> p (t i)").bitcast(I32))
+
+        def load_w1(g, a):
+            src = w1[a * KP:(a + 1) * KP, g * KP:(g + 1) * KP].rearrange("(p j) c -> p j c", j=PACK)
+            nc.sync.dma_start(raw[a][:].rearrange("p (j c) -> p j c", j=PACK), src)
+
+        def load_wgs(t, cols):
+            for q in (0, 2, 1, 3):
+                nc.sync.dma_start(wgs_sb[t][32 * q:32 * (q + 1), cols], wgs_v[t][:, cols])
+
+        def load_page(s):
+            nc.sync.dma_start(page[s][:], page0_v[s // PACK][s % PACK])
+
+        def quantise(codes, scales, src):
+            nc.vector.quantize_mx(out=codes.bitcast(FP8X4), scales=scales, in_=src)
+
+        def prep_w1(g, a, split=P):
+            st = stage[(PASSES * g + a) % 4]
+            dst = st[:].rearrange("p (t m j) -> p m j t", t=PACK, j=PACK)
+            src = raw[a][:].rearrange("p (j m t) -> p m j t", j=PACK, t=PACK)
+            nc.scalar.activation(out=dst[:, :split], in_=src[:, :split], func=ACT.Copy)
+            if split < P:
+                nc.vector.tensor_copy(dst[:, split:], src[:, split:])
+            quantise(w1c[g, a][:], w1s[g][a][:], st[:])
+
+        def prep_w3():
+            st = stage[2]
+            for g in range(GROUPS):
+                cols = slice(g * PACK * N, (g + 1) * PACK * N)
+                nc.scalar.activation(
+                    out=st[:, cols].rearrange("p (c i j) -> p c j i", i=4, j=PACK),
+                    in_=raw[0][:, cols].rearrange("p (j c i) -> p c j i", i=4, j=PACK), func=ACT.Copy)
+            quantise(late["w3c"][:], w3s[:], st[:])
+
+        def h_of(s):
+            return hbuf[s % 2 if s < 3 else 2 + s % 2]
+
+        def z_bank(s, hf):
+            return banks[hf if s > 1 else 0]
+
+        def z_matmuls(s, hf):
+            g, t = divmod(s, PACK)
+            cols = slice(t * P, (t + 1) * P)
+            for a in range(PASSES):
+                nc.tensor.matmul_mx(
+                    out=z_bank(s, hf)[:],
+                    lhsT=w1c[g, a][:, cols].bitcast(FP8X4), lhsT_scale=w1s[g][a][:, cols],
+                    rhs=vw[a][:, half(hf)].bitcast(FP8X4), rhs_scale=vs[4 * a:P, half(hf)],
+                    start=(a == 0), stop=(a == PASSES - 1))
+
+        def z_abs(s, hf):
+            nc.scalar.activation(out=h_of(s)[:, half(hf)], in_=z_bank(s, hf)[:], func=ACT.Abs)
+
+        def gained(s, hf):
+            cols = half(hf)
+            g, t = divmod(s, PACK)
+            nc.scalar.activation(out=h_of(s)[:, cols], in_=h_of(s)[:, cols], func=ACT.Copy,
+                                 scale=gain_sb[:, g, t:t + 1])
+
+        def z_exp(s, hf):
+            cols = half(hf)
+            nc.scalar.activation(out=h_of(s)[:, cols], in_=h_of(s)[:, cols], func=ACT.Exp, scale=-1.0)
+
+        def scatter(s, cols, list_cols):
+            nc.vector.tensor_tensor(page[s][:].indirect(idx2[:, list_cols]), h_of(s)[:, cols],
+                                    wgs_sb[s % PACK][:, cols], ALU.mult)
+
+        def quad_of(g, c):
+            return quad[(g * CHUNKS + c) % 6]
+
+        def regroup(s, chunks):
+            g, t = divmod(s, PACK)
+            for c in chunks:
+                nc.sync.dma_start(quad_of(g, c)[:, t, :], page[s][:, half(c)])
+
+        def store_page(s):
+            nc.sync.dma_start(out1_v[s // PACK][s % PACK], page[s][:])
+
+        def gather_x(s, cols, list_cols):
+            nc.vector.tensor_copy(xg[s % 2][:, cols], page[s][:].indirect(idx3[:, list_cols]))
+
+        def round_x(s, cols):
+            g, t = divmod(s, PACK)
+            nc.scalar.activation(out=xil[g][:, t, cols], in_=xg[s % 2][:, cols],
+                                 func=ACT.Identity, bias=bias_sb[:, g, t:t + 1])
+
+        def quantise_x(g, hf, on_vector, st):
+            dst = st[:].rearrange("p (c i t) -> p c t i", i=4, t=PACK)
+            src = xil[g][:, :, half(hf)].rearrange("p t (c i) -> p c t i", i=4)
+            if on_vector:
+                nc.vector.tensor_copy(dst, src)
+            else:
+                nc.scalar.activation(out=dst, in_=src, func=ACT.Copy)
+            quantise(xc[g, hf][:], xs[g][:, half(hf)], st[:])
+
+        def weave_x_early(hf, st):
+            dst = st[:].rearrange("p (c i t) -> p c t i", i=4, t=PACK)[:, :, :PACK - 1, :]
+            src = xil[1][:, :PACK - 1, half(hf)].rearrange("p t (c i) -> p c t i", i=4)
+            nc.scalar.activation(out=dst, in_=src, func=ACT.Copy)
+
+        def last_x(hf, st):
+            nc.scalar.activation(out=st[:].rearrange("p (j t) -> p j t", t=PACK)[:, :, PACK - 1],
+                                 in_=xg[1][:, half(hf)], func=ACT.Identity, bias=bias_sb[:, 1, PACK - 1:PACK])
+            quantise(xc[1, hf][:], xs[1][:, half(hf)], st[:])
+
+        def y_bank(hf, n, which):
+            return banks[(2 + 4 * hf + 2 * n + which) % 8]
+
+        def y_matmuls(g, hf):
+            moving = dict(rhs=xc[g, hf][:].bitcast(FP8X4), rhs_scale=xs[g][:, half(hf)],
+                          start=(g == 0), stop=(g == GROUPS - 1))
+            for n in range(NCH):
+                nc.tensor.matmul_mx(out=y_bank(hf, n, 0)[:], lhsT=w4c[:, g, 2 * P * n:2 * P * (n + 1)].bitcast(FP4X4),
+                                    lhsT_scale=w4s[:, g, P * n:P * (n + 1)], **moving)
+                cols = slice(g * N + P * n, g * N + P * (n + 1))
+                nc.tensor.matmul_mx(out=y_bank(hf, n, 1)[:], lhsT=late["w3c"][:, cols].bitcast(FP8X4), lhsT_scale=w3s[:, cols],
+                                    **moving)
+
+        def y_out(hf):
+            for n in range(NCH):
+                nc.scalar.activation(out=late["y", hf][:, half(n)], in_=y_bank(hf, n, 0)[:], func=ACT.Copy)
+            for n in range(NCH):
+                nc.vector.tensor_tensor(late["y", hf][:, half(n)], y_bank(hf, n, 1)[:], late["y", hf][:, half(n)], ALU.max)
+                nc.sync.dma_start(out_0[n * P:(n + 1) * P, half(hf)], late["y", hf][:, half(n)])
+
+        def planes_chunk(g, c, on_vector, st):
+            dst = st[:].rearrange("p (c i t) -> p c t i", i=4, t=PACK)
+            src = quad_of(g, c)[:].rearrange("p t (c i) -> p c t i", i=4)
+            if on_vector:
+                nc.vector.tensor_copy(dst, src)
+            else:
+                nc.scalar.activation(out=dst, in_=src, func=ACT.Copy)
+            quantise(planes_c[g, c][:], planes_s[g][:, half(c)], st[:])
+
+        def store_planes(g, c):
+            words = out_2[g].rearrange("p m t -> p (m t)").bitcast(I32)
+            nc.sync.dma_start(words[:, half(c)], planes_c[g, c][:].bitcast(I32))
+
+        def store_plane_scales(g):
+            for q in range(4):
+                nc.sync.dma_start(out_3[g][4 * q:4 * q + 4, :].bitcast(I32),
+                                  planes_s[g][32 * q:32 * q + 4, :].bitcast(I32))
+
+        whole = slice(0, S)
+        whole_list = slice(0, S // 16)
+
+        def signal(s):
+            for hf in range(2):
+                z_matmuls(s, hf)
+                z_abs(s, hf)
+            for step in (z_exp, gained):
+                for hf in range(2):
+                    step(s, hf)
+            scatter(s, whole, whole_list)
+
+        nc.vector.memset(tabs[:].bitcast(I32), 0)
+        nc.vector.memset(w4s[:].rearrange("p g n -> p (g n)").bitcast(I32), 0)
+        nc.sync.dma_start(idx[:], offs)
+        load_table(0)
+        load_w1(0, 0)
+        for q in range(4):
+            nc.sync.dma_start(tabs[32 * q:32 * q + 4 * PASSES, :].bitcast(I32),
+                              tab_scales[:, 4 * q:4 * q + 4, :].bitcast(I32))
+        nc.sync.dma_start(gain_sb[:], gain.rearrange("(g p t) -> p g t", g=GROUPS, t=PACK))
+        load_w1(0, 1)
+        load_w1(0, 2)
+        nc.sync.dma_start(idx2[:], offs2)
+        load_table(1)
+        nc.sync.dma_start(idx3[:], offs3)
+        load_table(2)
+        load_wgs(0, half(0))
+        load_page(0)
+        load_wgs(0, half(1))
+        load_wgs(1, whole)
+        load_page(1)
+
+        nc.vector.tensor_copy(vw[0][:], tabw[0][:].indirect(idx[:]))
+        prep_w1(0, 0, 48)
+        nc.vector.tensor_copy(vs[:], tabs[:].indirect(idx[:]))
+        prep_w1(0, 1, 48)
+        prep_w1(0, 2, 48)
+        nc.vector.tensor_copy(vw[1][:], tabw[1][:].indirect(idx[:]))
+        for hf in range(2):
+            nc.vector.tensor_copy(vw[2][:, half(hf)], tabw[2][:].indirect(idx[:, list_half(hf)]))
+
+        load_w1(1, 0)
+        load_wgs(2, whole)
+        load_w1(1, 1)
+        load_page(2)
+        load_w1(1, 2)
+        nc.sync.dma_start(bias_sb[:], bias.rearrange("(g p t) -> p g t", g=GROUPS, t=PACK))
+        load_wgs(3, whole)
+        load_page(3)
+
+        for hf in range(2):
+            z_matmuls(0, hf)
+            for step in (z_abs, z_exp, gained):
+                step(0, hf)
+            scatter(0, half(hf), list_half(hf))
+        quad[3] = tile("quad3", [P, PACK, HALF], F32, tag="tabw0")
+        quad[5] = tile("quad5", [P, PACK, HALF], F32, tag="tabw2")
+        planes_g1 = tile("planes_c1", [P, T2], U32, tag="tabw1")
+        for c in range(CHUNKS):
+            planes_c[1, c] = planes_g1[:, half(c)]
+        planes_s[0] = tile("planes_s0", [P, T2], U8, tag="tabs")
+
+        every = range(CHUNKS)
+        gather_x(0, whole, whole_list)
+        signal(1)
+        gather_x(1, whole, whole_list)
+        signal(2)
+        signal(3)
+        w1c[1, 0] = tile("w1c10", [P, KP], U32, tag="h1")
+        pair = tile("w1c11", [P, 2, KP], U32, tag="h0")
+        w1c[1, 1] = pair[:, 0, :]
+        w1c[1, 2] = pair[:, 1, :]
+        for a in range(PASSES):
+            prep_w1(1, a)
+        xil[0] = tile("xil0", [P, PACK, PX], BF16, tag="raw2")
+        xil[1] = tile("xil1", [P, PACK, PX], BF16, tag="raw1")
+        nc.sync.dma_start(raw[0][:].rearrange("p (g x) -> p g x", g=GROUPS),
+                          w3.rearrange("(g p j) n -> p g (j n)", g=GROUPS, j=PACK))
+        regroup(0, every)
+        regroup(1, every)
+        load_page(4)
+        regroup(2, every)
+        store_page(0)
+        regroup(3, every)
+        load_page(5)
+        store_page(1)
+        load_page(6)
+        store_page(2)
+        load_page(7)
+        nc.sync.dma_start(w4c[:].bitcast(I32), w4_words.rearrange("g p b -> p g b").bitcast(I32))
+        for q in range(4):
+            nc.sync.dma_start(w4s[32 * q:32 * q + 4, :, :].bitcast(I32),
+                              w4_scales[:, 4 * q:4 * q + 4, :].rearrange("g r n -> r g n").bitcast(I32))
+        store_page(3)
+        round_x(0, whole)
+        gather_x(2, whole, whole_list)
+        round_x(1, whole)
+        gather_x(3, whole, whole_list)
+        signal(4)
+        late["w3c"] = tile("w3c", [P, GROUPS * N], U32, tag="wgs0")
+        prep_w3()
+        quad[4] = tile("quad4", [P, PACK, HALF], F32, tag="raw0")
+        round_x(2, whole)
+        gather_x(4, whole, whole_list)
+        signal(5)
+        planes_c[0, 0] = tile("planes_c00", [P, HALF], U32, tag="wgs1")
+        round_x(3, whole)
+        gather_x(5, whole, whole_list)
+        signal(6)
+        signal(7)
+        pair = tile("xc0", [P, 2, HALF], U32, tag="h3")
+        xc[0, 0] = pair[:, 0, :]
+        xc[0, 1] = pair[:, 1, :]
+        pair = tile("planes_c01", [P, 3, HALF], U32, tag="wgs3")
+        for c in range(1, CHUNKS):
+            planes_c[0, c] = pair[:, c - 1, :]
+        regroup(4, (0, 1))
+        store_page(4)
+        regroup(5, (0, 1))
+        round_x(4, whole)
+        gather_x(6, whole, whole_list)
+        round_x(5, whole)
+        for hf in range(2):
+            gather_x(7, half(hf), list_half(hf))
+        round_x(6, whole)
+        pair = tile("xc1", [P, 2, HALF], U32, tag="h0")
+        for hf in range(2):
+            xc[1, hf] = pair[:, hf, :]
+            weave_x_early(hf, stage[5 + hf])
+        for hf in range(2):
+            last_x(hf, stage[5 + hf])
+        quantise_x(0, 0, False, stage[3])
+        quantise_x(0, 1, False, stage[0])
+        planes_chunk(0, 0, False, stage[1])
+        store_planes(0, 0)
+        regroup(4, (2,))
+        regroup(5, (2,))
+        store_page(5)
+        regroup(6, (0, 1, 2))
+        planes_chunk(0, 1, False, stage[2])
+        for s in (4, 5, 6):
+            regroup(s, (3,))
+        store_page(6)
+        regroup(7, (0, 2, 3))
+        store_page(7)
+        regroup(7, (1,))
+        for g in range(GROUPS):
+            y_matmuls(g, 0)
+        for g in range(GROUPS):
+            y_matmuls(g, 1)
+        store_planes(0, 1)
+        planes_chunk(0, 2, False, stage[4])
+        planes_chunk(0, 3, False, stage[1])
+        for c in (2, 3):
+            store_planes(0, c)
+        store_plane_scales(0)
+        planes_chunk(1, 0, False, stage[3])
+        planes_chunk(1, 1, False, stage[0])
+        planes_chunk(1, 2, True, stage[2])
+        planes_chunk(1, 3, True, stage[4])
+        for c in (0, 2, 3):
+            store_planes(1, c)
+        late["y", 0] = tile("y0", [P, PX], F32, tag="raw0")
+        late["y", 1] = tile("y1", [P, PX], F32, tag="tabw2")
+        y_out(0)
+        store_planes(1, 1)
+        store_plane_scales(1)
+        y_out(1)

@@ -1,6 +1,7 @@
 from contextlib import ExitStack
 
 import concourse.mybir as mybir
+from concourse.masks import make_identity
 
 K, H, N, T, S, T2, PX = 1536, 1024, 256, 2048, 1024, 2048, 1024
 FLOPS = 2 * K * H * S + 2 * 2 * H * N * PX
@@ -26,6 +27,7 @@ HALF = 512
 LIST_HALF = HALF // 16
 CHUNKS = T2 // HALF
 NCH = N // P
+FIRST = (slice(0, 256), slice(256, 512), slice(512, 1024))
 
 
 def tile_list_herbal_alert_scores_kernel(
@@ -73,13 +75,15 @@ def tile_list_herbal_alert_scores_kernel(
         xc = {}
         xs = [tile("xs%d" % g, [P, PX], U8) for g in range(GROUPS)]
         planes_s = {1: tile("planes_s1", [P, T2], U8)}
-        quad = {c: tile("quad%d" % c, [P, PACK, HALF], F32) for c in range(3)}
+        quad = {}
+        ident = tile("ident", [P, P], F32)
+        wgs_rows = tile("wgs_rows", [P, S], F32, tag="quad2")
+        wgs_t = [tile("wgs_t%d" % hf, [P, 4, PACK, 4, 32], F32, tag="quad%d" % hf) for hf in range(2)]
         planes_c = {}
         xil = {}
 
         page0_v = page0.rearrange("(g p t) m -> g t p m", g=GROUPS, t=PACK)
         out1_v = out_1.rearrange("(g p t) m -> g t p m", g=GROUPS, t=PACK)
-        wgs_v = wgs.rearrange("(q t) j -> t q j", t=PACK)
 
         def load_table(a):
             nc.sync.dma_start(tabw[a][:].bitcast(I32), tab_words[a].rearrange("p t i -> p (t i)").bitcast(I32))
@@ -88,9 +92,21 @@ def tile_list_herbal_alert_scores_kernel(
             src = w1[a * KP:(a + 1) * KP, g * KP:(g + 1) * KP].rearrange("(p j) c -> p j c", j=PACK)
             nc.sync.dma_start(raw[a][:].rearrange("p (j c) -> p j c", j=PACK), src)
 
-        def load_wgs(t, cols):
-            for q in (0, 2, 1, 3):
-                nc.sync.dma_start(wgs_sb[t][32 * q:32 * (q + 1), cols], wgs_v[t][:, cols])
+        def turn_wgs(hf):
+            bank = banks[2 + hf]
+            for c in range(4):
+                nc.tensor.transpose(bank[:, c * P:(c + 1) * P], wgs_rows[:, hf * HALF + c * P:hf * HALF + (c + 1) * P],
+                                    ident[:])
+            for q in range(4):
+                nc.scalar.activation(out=wgs_t[hf][:, :, :, q, :],
+                                     in_=bank[:].rearrange("j (c r t) -> j c t r", c=4, t=PACK), func=ACT.Copy)
+
+        def deal_wgs(t, hf):
+            bank = banks[4 + (2 * t + hf) % 4]
+            for c in range(4):
+                nc.tensor.transpose(bank[:, c * P:(c + 1) * P], wgs_t[hf][:, c, t, :, :].rearrange("j q r -> j (q r)"),
+                                    ident[:])
+            nc.scalar.activation(out=wgs_sb[t][:, half(hf)], in_=bank[:], func=ACT.Copy)
 
         def load_page(s):
             nc.sync.dma_start(page[s][:], page0_v[s // PACK][s % PACK])
@@ -102,9 +118,13 @@ def tile_list_herbal_alert_scores_kernel(
             st = stage[(PASSES * g + a) % 4]
             dst = st[:].rearrange("p (t m j) -> p m j t", t=PACK, j=PACK)
             src = raw[a][:].rearrange("p (j m t) -> p m j t", j=PACK, t=PACK)
-            nc.scalar.activation(out=dst[:, :split], in_=src[:, :split], func=ACT.Copy)
+            if split > 0:
+                nc.scalar.activation(out=dst[:, :split], in_=src[:, :split], func=ACT.Copy)
             if split < P:
                 nc.vector.tensor_copy(dst[:, split:], src[:, split:])
+
+        def quantise_w1(g, a):
+            st = stage[(PASSES * g + a) % 4]
             quantise(w1c[g, a][:], w1s[g][a][:], st[:])
 
         def prep_w3():
@@ -114,35 +134,36 @@ def tile_list_herbal_alert_scores_kernel(
                 nc.scalar.activation(
                     out=st[:, cols].rearrange("p (c i j) -> p c j i", i=4, j=PACK),
                     in_=raw[0][:, cols].rearrange("p (j c i) -> p c j i", i=4, j=PACK), func=ACT.Copy)
+
+        def quantise_w3():
+            st = stage[2]
             quantise(late["w3c"][:], w3s[:], st[:])
 
         def h_of(s):
             return hbuf[s % 2 if s < 3 else 2 + s % 2]
 
         def z_bank(s, hf):
-            return banks[hf if s > 1 else 0]
+            return banks[hf if s > 1 else 3 + hf]
 
-        def z_matmuls(s, hf):
+        def z_matmuls(s, bank, picks):
             g, t = divmod(s, PACK)
             cols = slice(t * P, (t + 1) * P)
             for a in range(PASSES):
                 nc.tensor.matmul_mx(
-                    out=z_bank(s, hf)[:],
+                    out=bank[:, :picks.stop - picks.start],
                     lhsT=w1c[g, a][:, cols].bitcast(FP8X4), lhsT_scale=w1s[g][a][:, cols],
-                    rhs=vw[a][:, half(hf)].bitcast(FP8X4), rhs_scale=vs[4 * a:P, half(hf)],
+                    rhs=vw[a][:, picks].bitcast(FP8X4), rhs_scale=vs[4 * a:P, picks],
                     start=(a == 0), stop=(a == PASSES - 1))
 
-        def z_abs(s, hf):
-            nc.scalar.activation(out=h_of(s)[:, half(hf)], in_=z_bank(s, hf)[:], func=ACT.Abs)
+        def z_abs(s, bank, picks):
+            nc.scalar.activation(out=h_of(s)[:, picks], in_=bank[:, :picks.stop - picks.start], func=ACT.Abs)
 
-        def gained(s, hf):
-            cols = half(hf)
+        def gained(s, cols):
             g, t = divmod(s, PACK)
             nc.scalar.activation(out=h_of(s)[:, cols], in_=h_of(s)[:, cols], func=ACT.Copy,
                                  scale=gain_sb[:, g, t:t + 1])
 
-        def z_exp(s, hf):
-            cols = half(hf)
+        def z_exp(s, cols):
             nc.scalar.activation(out=h_of(s)[:, cols], in_=h_of(s)[:, cols], func=ACT.Exp, scale=-1.0)
 
         def scatter(s, cols, list_cols):
@@ -168,13 +189,15 @@ def tile_list_herbal_alert_scores_kernel(
             nc.scalar.activation(out=xil[g][:, t, cols], in_=xg[s % 2][:, cols],
                                  func=ACT.Identity, bias=bias_sb[:, g, t:t + 1])
 
-        def quantise_x(g, hf, on_vector, st):
+        def weave_x(g, hf, on_vector, st):
             dst = st[:].rearrange("p (c i t) -> p c t i", i=4, t=PACK)
             src = xil[g][:, :, half(hf)].rearrange("p t (c i) -> p c t i", i=4)
             if on_vector:
                 nc.vector.tensor_copy(dst, src)
             else:
                 nc.scalar.activation(out=dst, in_=src, func=ACT.Copy)
+
+        def quantise_x(g, hf, st):
             quantise(xc[g, hf][:], xs[g][:, half(hf)], st[:])
 
         def weave_x_early(hf, st):
@@ -207,13 +230,15 @@ def tile_list_herbal_alert_scores_kernel(
                 nc.vector.tensor_tensor(late["y", hf][:, half(n)], y_bank(hf, n, 1)[:], late["y", hf][:, half(n)], ALU.max)
                 nc.sync.dma_start(out_0[n * P:(n + 1) * P, half(hf)], late["y", hf][:, half(n)])
 
-        def planes_chunk(g, c, on_vector, st):
+        def weave_page(g, c, on_vector, st):
             dst = st[:].rearrange("p (c i t) -> p c t i", i=4, t=PACK)
             src = quad_of(g, c)[:].rearrange("p t (c i) -> p c t i", i=4)
             if on_vector:
                 nc.vector.tensor_copy(dst, src)
             else:
                 nc.scalar.activation(out=dst, in_=src, func=ACT.Copy)
+
+        def quantise_page(g, c, st):
             quantise(planes_c[g, c][:], planes_s[g][:, half(c)], st[:])
 
         def store_planes(g, c):
@@ -230,15 +255,17 @@ def tile_list_herbal_alert_scores_kernel(
 
         def signal(s):
             for hf in range(2):
-                z_matmuls(s, hf)
-                z_abs(s, hf)
+                z_matmuls(s, z_bank(s, hf), half(hf))
+                z_abs(s, z_bank(s, hf), half(hf))
             for step in (z_exp, gained):
                 for hf in range(2):
-                    step(s, hf)
+                    step(s, half(hf))
             scatter(s, whole, whole_list)
 
         nc.vector.memset(tabs[:].bitcast(I32), 0)
         nc.vector.memset(w4s[:].rearrange("p g n -> p (g n)").bitcast(I32), 0)
+        make_identity(nc, ident[:])
+        nc.sync.dma_start(wgs_rows[:], wgs)
         nc.sync.dma_start(idx[:], offs)
         load_table(0)
         load_w1(0, 0)
@@ -247,40 +274,46 @@ def tile_list_herbal_alert_scores_kernel(
                               tab_scales[:, 4 * q:4 * q + 4, :].bitcast(I32))
         nc.sync.dma_start(gain_sb[:], gain.rearrange("(g p t) -> p g t", g=GROUPS, t=PACK))
         load_w1(0, 1)
-        load_w1(0, 2)
-        nc.sync.dma_start(idx2[:], offs2)
         load_table(1)
+        nc.sync.dma_start(idx2[:], offs2)
+        load_w1(0, 2)
         nc.sync.dma_start(idx3[:], offs3)
         load_table(2)
-        load_wgs(0, half(0))
         load_page(0)
-        load_wgs(0, half(1))
-        load_wgs(1, whole)
         load_page(1)
 
-        nc.vector.tensor_copy(vw[0][:], tabw[0][:].indirect(idx[:]))
-        prep_w1(0, 0, 48)
-        nc.vector.tensor_copy(vs[:], tabs[:].indirect(idx[:]))
-        prep_w1(0, 1, 48)
-        prep_w1(0, 2, 48)
-        nc.vector.tensor_copy(vw[1][:], tabw[1][:].indirect(idx[:]))
         for hf in range(2):
-            nc.vector.tensor_copy(vw[2][:, half(hf)], tabw[2][:].indirect(idx[:, list_half(hf)]))
+            turn_wgs(hf)
+        nc.vector.tensor_copy(vw[0][:], tabw[0][:].indirect(idx[:]))
+        prep_w1(0, 0, 0)
+        quantise_w1(0, 0)
+        nc.vector.tensor_copy(vs[:], tabs[:].indirect(idx[:]))
+        prep_w1(0, 1, 0)
+        quantise_w1(0, 1)
+        nc.vector.tensor_copy(vw[1][:], tabw[1][:].indirect(idx[:]))
+        prep_w1(0, 2, 48)
+        quantise_w1(0, 2)
+        for picks in FIRST:
+            nc.vector.tensor_copy(vw[2][:, picks], tabw[2][:].indirect(idx[:, picks.start // 16:picks.stop // 16]))
 
+        for t in range(PACK):
+            for hf in range(2):
+                deal_wgs(t, hf)
+        for c in range(3):
+            quad[c] = tile("quad%d" % c, [P, PACK, HALF], F32)
         load_w1(1, 0)
-        load_wgs(2, whole)
         load_w1(1, 1)
         load_page(2)
         load_w1(1, 2)
         nc.sync.dma_start(bias_sb[:], bias.rearrange("(g p t) -> p g t", g=GROUPS, t=PACK))
-        load_wgs(3, whole)
         load_page(3)
 
-        for hf in range(2):
-            z_matmuls(0, hf)
-            for step in (z_abs, z_exp, gained):
-                step(0, hf)
-            scatter(0, half(hf), list_half(hf))
+        for bank, picks in zip(banks, FIRST):
+            z_matmuls(0, bank, picks)
+            z_abs(0, bank, picks)
+            z_exp(0, picks)
+            gained(0, picks)
+            scatter(0, picks, slice(picks.start // 16, picks.stop // 16))
         quad[3] = tile("quad3", [P, PACK, HALF], F32, tag="tabw0")
         quad[5] = tile("quad5", [P, PACK, HALF], F32, tag="tabw2")
         planes_g1 = tile("planes_c1", [P, T2], U32, tag="tabw1")
@@ -293,33 +326,34 @@ def tile_list_herbal_alert_scores_kernel(
         signal(1)
         gather_x(1, whole, whole_list)
         signal(2)
-        signal(3)
         w1c[1, 0] = tile("w1c10", [P, KP], U32, tag="h1")
         pair = tile("w1c11", [P, 2, KP], U32, tag="h0")
         w1c[1, 1] = pair[:, 0, :]
         w1c[1, 2] = pair[:, 1, :]
         for a in range(PASSES):
             prep_w1(1, a)
+            quantise_w1(1, a)
+        signal(3)
         xil[0] = tile("xil0", [P, PACK, PX], BF16, tag="raw2")
         xil[1] = tile("xil1", [P, PACK, PX], BF16, tag="raw1")
         nc.sync.dma_start(raw[0][:].rearrange("p (g x) -> p g x", g=GROUPS),
                           w3.rearrange("(g p j) n -> p g (j n)", g=GROUPS, j=PACK))
         regroup(0, every)
         regroup(1, every)
+        store_page(0)
         load_page(4)
         regroup(2, every)
-        store_page(0)
+        store_page(1)
         regroup(3, every)
         load_page(5)
-        store_page(1)
-        load_page(6)
         store_page(2)
+        load_page(6)
+        store_page(3)
         load_page(7)
         nc.sync.dma_start(w4c[:].bitcast(I32), w4_words.rearrange("g p b -> p g b").bitcast(I32))
         for q in range(4):
             nc.sync.dma_start(w4s[32 * q:32 * q + 4, :, :].bitcast(I32),
                               w4_scales[:, 4 * q:4 * q + 4, :].rearrange("g r n -> r g n").bitcast(I32))
-        store_page(3)
         round_x(0, whole)
         gather_x(2, whole, whole_list)
         round_x(1, whole)
@@ -327,6 +361,7 @@ def tile_list_herbal_alert_scores_kernel(
         signal(4)
         late["w3c"] = tile("w3c", [P, GROUPS * N], U32, tag="wgs0")
         prep_w3()
+        quantise_w3()
         quad[4] = tile("quad4", [P, PACK, HALF], F32, tag="raw0")
         round_x(2, whole)
         gather_x(4, whole, whole_list)
@@ -334,19 +369,27 @@ def tile_list_herbal_alert_scores_kernel(
         planes_c[0, 0] = tile("planes_c00", [P, HALF], U32, tag="wgs1")
         round_x(3, whole)
         gather_x(5, whole, whole_list)
+        weave_x(0, 0, False, stage[3])
+        weave_x(0, 1, False, stage[0])
+        weave_page(0, 0, False, stage[1])
+        quantise_page(0, 0, stage[1])
         signal(6)
-        signal(7)
-        pair = tile("xc0", [P, 2, HALF], U32, tag="h3")
+        pair = tile("planes_c01", [P, HALF], U32, tag="wgs2")
+        planes_c[0, 1] = pair
+        pair = tile("xc0", [P, 2, HALF], U32, tag="h2")
         xc[0, 0] = pair[:, 0, :]
         xc[0, 1] = pair[:, 1, :]
-        pair = tile("planes_c01", [P, 3, HALF], U32, tag="wgs3")
-        for c in range(1, CHUNKS):
-            planes_c[0, c] = pair[:, c - 1, :]
-        regroup(4, (0, 1))
-        store_page(4)
-        regroup(5, (0, 1))
+        quantise_x(0, 0, stage[3])
+        quantise_x(0, 1, stage[0])
         round_x(4, whole)
         gather_x(6, whole, whole_list)
+        weave_page(0, 1, False, stage[2])
+        quantise_page(0, 1, stage[2])
+        weave_page(0, 2, False, stage[4])
+        signal(7)
+        pair = tile("planes_c02", [P, 2, HALF], U32, tag="wgs3")
+        for c in (2, 3):
+            planes_c[0, c] = pair[:, c - 2, :]
         round_x(5, whole)
         for hf in range(2):
             gather_x(7, half(hf), list_half(hf))
@@ -355,19 +398,22 @@ def tile_list_herbal_alert_scores_kernel(
         for hf in range(2):
             xc[1, hf] = pair[:, hf, :]
             weave_x_early(hf, stage[5 + hf])
+        weave_page(0, 3, False, stage[1])
         for hf in range(2):
             last_x(hf, stage[5 + hf])
-        quantise_x(0, 0, False, stage[3])
-        quantise_x(0, 1, False, stage[0])
-        planes_chunk(0, 0, False, stage[1])
-        store_planes(0, 0)
+        quantise_page(0, 2, stage[4])
+        quantise_page(0, 3, stage[1])
+        regroup(4, (0, 1))
+        store_page(4)
+        regroup(5, (0, 1))
         regroup(4, (2,))
         regroup(5, (2,))
+        store_planes(0, 0)
         store_page(5)
         regroup(6, (0, 1, 2))
-        planes_chunk(0, 1, False, stage[2])
         for s in (4, 5, 6):
             regroup(s, (3,))
+        store_planes(0, 1)
         store_page(6)
         regroup(7, (0, 2, 3))
         store_page(7)
@@ -376,16 +422,12 @@ def tile_list_herbal_alert_scores_kernel(
             y_matmuls(g, 0)
         for g in range(GROUPS):
             y_matmuls(g, 1)
-        store_planes(0, 1)
-        planes_chunk(0, 2, False, stage[4])
-        planes_chunk(0, 3, False, stage[1])
-        for c in (2, 3):
-            store_planes(0, c)
+        store_planes(0, 2)
+        store_planes(0, 3)
         store_plane_scales(0)
-        planes_chunk(1, 0, False, stage[3])
-        planes_chunk(1, 1, False, stage[0])
-        planes_chunk(1, 2, True, stage[2])
-        planes_chunk(1, 3, True, stage[4])
+        for c, st in ((0, 3), (1, 0), (2, 2), (3, 4)):
+            weave_page(1, c, c >= 2, stage[st])
+            quantise_page(1, c, stage[st])
         for c in (0, 2, 3):
             store_planes(1, c)
         late["y", 0] = tile("y0", [P, PX], F32, tag="raw0")

@@ -132,8 +132,8 @@ def tile_list_herbal_alert_scores_kernel(
             for g in range(GROUPS):
                 cols = slice(g * PACK * N, (g + 1) * PACK * N)
                 nc.scalar.activation(
-                    out=st[:, cols].rearrange("p (c i j) -> p c j i", i=4, j=PACK),
-                    in_=raw[0][:, cols].rearrange("p (j c i) -> p c j i", i=4, j=PACK), func=ACT.Copy)
+                    out=st[:, cols].rearrange("p (c i j) -> p c j i", i=2, j=PACK),
+                    in_=raw[0][:, cols].rearrange("p (j c i) -> p c j i", i=2, j=PACK), func=ACT.Copy)
 
         def quantise_w3():
             st = stage[2]
@@ -190,8 +190,8 @@ def tile_list_herbal_alert_scores_kernel(
                                  func=ACT.Identity, bias=bias_sb[:, g, t:t + 1])
 
         def weave_x(g, hf, on_vector, st):
-            dst = st[:].rearrange("p (c i t) -> p c t i", i=4, t=PACK)
-            src = xil[g][:, :, half(hf)].rearrange("p t (c i) -> p c t i", i=4)
+            dst = st[:].rearrange("p (c i t) -> p c t i", i=2, t=PACK)
+            src = xil[g][:, :, half(hf)].rearrange("p t (c i) -> p c t i", i=2)
             if on_vector:
                 nc.vector.tensor_copy(dst, src)
             else:
@@ -201,8 +201,8 @@ def tile_list_herbal_alert_scores_kernel(
             quantise(xc[g, hf][:], xs[g][:, half(hf)], st[:])
 
         def weave_x_early(hf, st):
-            dst = st[:].rearrange("p (c i t) -> p c t i", i=4, t=PACK)[:, :, :PACK - 1, :]
-            src = xil[1][:, :PACK - 1, half(hf)].rearrange("p t (c i) -> p c t i", i=4)
+            dst = st[:].rearrange("p (c i t) -> p c t i", i=2, t=PACK)[:, :, :PACK - 1, :]
+            src = xil[1][:, :PACK - 1, half(hf)].rearrange("p t (c i) -> p c t i", i=2)
             nc.scalar.activation(out=dst, in_=src, func=ACT.Copy)
 
         def last_x(hf, st):
@@ -231,8 +231,8 @@ def tile_list_herbal_alert_scores_kernel(
                 nc.sync.dma_start(out_0[n * P:(n + 1) * P, half(hf)], late["y", hf][:, half(n)])
 
         def weave_page(g, c, on_vector, st):
-            dst = st[:].rearrange("p (c i t) -> p c t i", i=4, t=PACK)
-            src = quad_of(g, c)[:].rearrange("p t (c i) -> p c t i", i=4)
+            dst = st[:].rearrange("p (c i t) -> p c t i", i=2, t=PACK)
+            src = quad_of(g, c)[:].rearrange("p t (c i) -> p c t i", i=2)
             if on_vector:
                 nc.vector.tensor_copy(dst, src)
             else:
@@ -265,13 +265,13 @@ def tile_list_herbal_alert_scores_kernel(
         nc.vector.memset(tabs[:].bitcast(I32), 0)
         nc.vector.memset(w4s[:].rearrange("p g n -> p (g n)").bitcast(I32), 0)
         make_identity(nc, ident[:])
-        nc.sync.dma_start(wgs_rows[:], wgs)
         nc.sync.dma_start(idx[:], offs)
         load_table(0)
-        load_w1(0, 0)
+        nc.sync.dma_start(wgs_rows[:], wgs)
         for q in range(4):
             nc.sync.dma_start(tabs[32 * q:32 * q + 4 * PASSES, :].bitcast(I32),
                               tab_scales[:, 4 * q:4 * q + 4, :].bitcast(I32))
+        load_w1(0, 0)
         nc.sync.dma_start(gain_sb[:], gain.rearrange("(g p t) -> p g t", g=GROUPS, t=PACK))
         load_w1(0, 1)
         load_table(1)
@@ -285,13 +285,13 @@ def tile_list_herbal_alert_scores_kernel(
         for hf in range(2):
             turn_wgs(hf)
         nc.vector.tensor_copy(vw[0][:], tabw[0][:].indirect(idx[:]))
+        nc.vector.tensor_copy(vs[:], tabs[:].indirect(idx[:]))
         prep_w1(0, 0, 0)
         quantise_w1(0, 0)
-        nc.vector.tensor_copy(vs[:], tabs[:].indirect(idx[:]))
         prep_w1(0, 1, 0)
         quantise_w1(0, 1)
         nc.vector.tensor_copy(vw[1][:], tabw[1][:].indirect(idx[:]))
-        prep_w1(0, 2, 48)
+        prep_w1(0, 2, 0)
         quantise_w1(0, 2)
         for picks in FIRST:
             nc.vector.tensor_copy(vw[2][:, picks], tabw[2][:].indirect(idx[:, picks.start // 16:picks.stop // 16]))

from contextlib import ExitStack

import concourse.mybir as mybir
from concourse.masks import make_identity

K, H, N, T, S, T2, PX = 1536, 1024, 256, 2048, 1024, 2048, 1024
FLOPS = 2 * K * H * S + 2 * 2 * H * N * PX

F32 = mybir.dt.float32
BF16 = mybir.dt.bfloat16
I32 = mybir.dt.int32
U32 = mybir.dt.uint32
U16 = mybir.dt.uint16
U8 = mybir.dt.uint8
FP8X4 = mybir.dt.float8_e4m3fn_x4
FP4X4 = mybir.dt.float4_e2m1fn_x4
ALU = mybir.AluOpType
ACT = mybir.ActivationFunctionType

P = 128
PACK = 4
KP = P * PACK
PASSES = K // KP
GROUPS = H // KP
SLICES = GROUPS * PACK
HALF = 512
LIST_HALF = HALF // 16
CHUNKS = T2 // HALF
NCH = N // P
FIRST = (slice(0, 256), slice(256, 512), slice(512, 1024))


def tile_list_herbal_alert_scores_kernel(
    tc, tab_words, tab_scales, offs, offs2, offs3, w1, gain, wgs, page0, bias, w4_words, w4_scales, w3,
    out_0, out_1, out_2, out_3,
):
    nc = tc.nc
    with ExitStack() as ctx:
        lists = ctx.enter_context(tc.tile_pool(name="lists", bufs=1))
        sb = ctx.enter_context(tc.tile_pool(name="sb", bufs=1))
        ps = ctx.enter_context(tc.psum_pool(name="ps", bufs=1))

        def tile(name, shape, dtype, tag=None):
            return sb.tile(shape, dtype, name=name, tag=tag or name, align_bytes=64)

        def half(i):
            return slice(i * HALF, (i + 1) * HALF)

        def list_half(i):
            return slice(i * LIST_HALF, (i + 1) * LIST_HALF)

        idx = lists.tile([P, S // 16], U16, name="idx")
        idx2 = lists.tile([P, S // 16], U16, name="idx2")
        idx3 = lists.tile([P, PX // 16], U16, name="idx3")
        banks = [ps.tile([P, HALF], F32, name="bank%d" % b) for b in range(8)]

        gain_sb = tile("gain_sb", [P, GROUPS, PACK], F32)
        bias_sb = tile("bias_sb", [P, GROUPS, PACK], F32)
        tabw = [tile("tabw%d" % a, [P, T], U32) for a in range(PASSES)]
        tabs = tile("tabs", [P, T], U8)
        vw = [tile("vw%d" % a, [P, S], U32) for a in range(PASSES)]
        vs = tile("vs", [P, S], U8)
        raw = [tile("raw%d" % a, [P, PACK * HALF], F32) for a in range(PASSES)]
        stage = [tile("stage%d" % i, [P, PACK * HALF], BF16) for i in range(7)]
        w1c = {(0, a): tile("w1c0%d" % a, [P, KP], U32) for a in range(PASSES)}
        w1s = [[tile("w1s%d%d" % (g, a), [P, KP], U8) for a in range(PASSES)] for g in range(GROUPS)]
        wgs_sb = [tile("wgs%d" % t, [P, S], F32) for t in range(PACK)]
        page = {s: tile("page%d" % s, [P, T2], F32) for s in range(SLICES)}
        w4c = tile("w4c", [P, GROUPS, 2 * N], U8)
        w4s = tile("w4s", [P, GROUPS, N], U8)
        w3s = tile("w3s", [P, GROUPS * N], U8)
        hbuf = [tile("h%d" % i, [P, S], F32) for i in range(4)]
        late = {}
        xg = [tile("xg%d" % i, [P, PX], F32) for i in range(2)]
        xc = {}
        xs = [tile("xs%d" % g, [P, PX], U8) for g in range(GROUPS)]
        planes_s = {1: tile("planes_s1", [P, T2], U8)}
        quad = {}
        ident = tile("ident", [P, P], F32)
        wgs_rows = tile("wgs_rows", [P, S], F32, tag="quad2")
        wgs_t = [tile("wgs_t%d" % hf, [P, 4, PACK, 4, 32], F32, tag="quad%d" % hf) for hf in range(2)]
        planes_c = {}
        xil = {}

        page0_v = page0.rearrange("(g p t) m -> g t p m", g=GROUPS, t=PACK)
        out1_v = out_1.rearrange("(g p t) m -> g t p m", g=GROUPS, t=PACK)

        def load_table(a):
            nc.sync.dma_start(tabw[a][:].bitcast(I32), tab_words[a].rearrange("p t i -> p (t i)").bitcast(I32))

        def load_w1(g, a):
            src = w1[a * KP:(a + 1) * KP, g * KP:(g + 1) * KP].rearrange("(p j) c -> p j c", j=PACK)
            nc.sync.dma_start(raw[a][:].rearrange("p (j c) -> p j c", j=PACK), src)

        def turn_wgs(hf):
            bank = banks[2 + hf]
            for c in range(4):
                nc.tensor.transpose(bank[:, c * P:(c + 1) * P], wgs_rows[:, hf * HALF + c * P:hf * HALF + (c + 1) * P],
                                    ident[:])
            for q in range(4):
                nc.scalar.activation(out=wgs_t[hf][:, :, :, q, :],
                                     in_=bank[:].rearrange("j (c r t) -> j c t r", c=4, t=PACK), func=ACT.Copy)

        def deal_wgs(t, hf):
            bank = banks[4 + (2 * t + hf) % 4]
            for c in range(4):
                nc.tensor.transpose(bank[:, c * P:(c + 1) * P], wgs_t[hf][:, c, t, :, :].rearrange("j q r -> j (q r)"),
                                    ident[:])
            nc.scalar.activation(out=wgs_sb[t][:, half(hf)], in_=bank[:], func=ACT.Copy)

        def load_page(s):
            nc.sync.dma_start(page[s][:], page0_v[s // PACK][s % PACK])

        def quantise(codes, scales, src):
            nc.vector.quantize_mx(out=codes.bitcast(FP8X4), scales=scales, in_=src)

        def prep_w1(g, a, split=P):
            st = stage[(PASSES * g + a) % 4]
            dst = st[:].rearrange("p (t m j) -> p m j t", t=PACK, j=PACK)
            src = raw[a][:].rearrange("p (j m t) -> p m j t", j=PACK, t=PACK)
            if split > 0:
                nc.scalar.activation(out=dst[:, :split], in_=src[:, :split], func=ACT.Copy)
            if split < P:
                nc.vector.tensor_copy(dst[:, split:], src[:, split:])

        def quantise_w1(g, a):
            st = stage[(PASSES * g + a) % 4]
            quantise(w1c[g, a][:], w1s[g][a][:], st[:])

        def prep_w3():
            st = stage[2]
            for g in range(GROUPS):
                cols = slice(g * PACK * N, (g + 1) * PACK * N)
                nc.scalar.activation(
                    out=st[:, cols].rearrange("p (c i j) -> p c j i", i=2, j=PACK),
                    in_=raw[0][:, cols].rearrange("p (j c i) -> p c j i", i=2, j=PACK), func=ACT.Copy)

        def quantise_w3():
            st = stage[2]
            quantise(late["w3c"][:], w3s[:], st[:])

        def h_of(s):
            return hbuf[s % 2 if s < 3 else 2 + s % 2]

        def z_bank(s, hf):
            return banks[hf if s > 1 else 3 + hf]

        def z_matmuls(s, bank, picks):
            g, t = divmod(s, PACK)
            cols = slice(t * P, (t + 1) * P)
            for a in range(PASSES):
                nc.tensor.matmul_mx(
                    out=bank[:, :picks.stop - picks.start],
                    lhsT=w1c[g, a][:, cols].bitcast(FP8X4), lhsT_scale=w1s[g][a][:, cols],
                    rhs=vw[a][:, picks].bitcast(FP8X4), rhs_scale=vs[4 * a:P, picks],
                    start=(a == 0), stop=(a == PASSES - 1))

        def z_abs(s, bank, picks):
            nc.scalar.activation(out=h_of(s)[:, picks], in_=bank[:, :picks.stop - picks.start], func=ACT.Abs)

        def gained(s, cols):
            g, t = divmod(s, PACK)
            nc.scalar.activation(out=h_of(s)[:, cols], in_=h_of(s)[:, cols], func=ACT.Copy,
                                 scale=gain_sb[:, g, t:t + 1])

        def z_exp(s, cols):
            nc.scalar.activation(out=h_of(s)[:, cols], in_=h_of(s)[:, cols], func=ACT.Exp, scale=-1.0)

        def scatter(s, cols, list_cols):
            nc.vector.tensor_tensor(page[s][:].indirect(idx2[:, list_cols]), h_of(s)[:, cols],
                                    wgs_sb[s % PACK][:, cols], ALU.mult)

        def quad_of(g, c):
            return quad[(g * CHUNKS + c) % 6]

        def regroup(s, chunks):
            g, t = divmod(s, PACK)
            for c in chunks:
                nc.sync.dma_start(quad_of(g, c)[:, t, :], page[s][:, half(c)])

        def store_page(s):
            nc.sync.dma_start(out1_v[s // PACK][s % PACK], page[s][:])

        def gather_x(s, cols, list_cols):
            nc.vector.tensor_copy(xg[s % 2][:, cols], page[s][:].indirect(idx3[:, list_cols]))

        def round_x(s, cols):
            g, t = divmod(s, PACK)
            nc.scalar.activation(out=xil[g][:, t, cols], in_=xg[s % 2][:, cols],
                                 func=ACT.Identity, bias=bias_sb[:, g, t:t + 1])

        def weave_x(g, hf, on_vector, st):
            dst = st[:].rearrange("p (c i t) -> p c t i", i=2, t=PACK)
            src = xil[g][:, :, half(hf)].rearrange("p t (c i) -> p c t i", i=2)
            if on_vector:
                nc.vector.tensor_copy(dst, src)
            else:
                nc.scalar.activation(out=dst, in_=src, func=ACT.Copy)

        def quantise_x(g, hf, st):
            quantise(xc[g, hf][:], xs[g][:, half(hf)], st[:])

        def weave_x_early(hf, st):
            dst = st[:].rearrange("p (c i t) -> p c t i", i=2, t=PACK)[:, :, :PACK - 1, :]
            src = xil[1][:, :PACK - 1, half(hf)].rearrange("p t (c i) -> p c t i", i=2)
            nc.scalar.activation(out=dst, in_=src, func=ACT.Copy)

        def last_x(hf, st):
            nc.scalar.activation(out=st[:].rearrange("p (j t) -> p j t", t=PACK)[:, :, PACK - 1],
                                 in_=xg[1][:, half(hf)], func=ACT.Identity, bias=bias_sb[:, 1, PACK - 1:PACK])
            quantise(xc[1, hf][:], xs[1][:, half(hf)], st[:])

        def y_bank(hf, n, which):
            return banks[(2 + 4 * hf + 2 * n + which) % 8]

        def y_matmuls(g, hf):
            moving = dict(rhs=xc[g, hf][:].bitcast(FP8X4), rhs_scale=xs[g][:, half(hf)],
                          start=(g == 0), stop=(g == GROUPS - 1))
            for n in range(NCH):
                nc.tensor.matmul_mx(out=y_bank(hf, n, 0)[:], lhsT=w4c[:, g, 2 * P * n:2 * P * (n + 1)].bitcast(FP4X4),
                                    lhsT_scale=w4s[:, g, P * n:P * (n + 1)], **moving)
                cols = slice(g * N + P * n, g * N + P * (n + 1))
                nc.tensor.matmul_mx(out=y_bank(hf, n, 1)[:], lhsT=late["w3c"][:, cols].bitcast(FP8X4), lhsT_scale=w3s[:, cols],
                                    **moving)

        def y_out(hf):
            for n in range(NCH):
                nc.scalar.activation(out=late["y", hf][:, half(n)], in_=y_bank(hf, n, 0)[:], func=ACT.Copy)
            for n in range(NCH):
                nc.vector.tensor_tensor(late["y", hf][:, half(n)], y_bank(hf, n, 1)[:], late["y", hf][:, half(n)], ALU.max)
                nc.sync.dma_start(out_0[n * P:(n + 1) * P, half(hf)], late["y", hf][:, half(n)])

        def weave_page(g, c, on_vector, st):
            dst = st[:].rearrange("p (c i t) -> p c t i", i=2, t=PACK)
            src = quad_of(g, c)[:].rearrange("p t (c i) -> p c t i", i=2)
            if on_vector:
                nc.vector.tensor_copy(dst, src)
            else:
                nc.scalar.activation(out=dst, in_=src, func=ACT.Copy)

        def quantise_page(g, c, st):
            quantise(planes_c[g, c][:], planes_s[g][:, half(c)], st[:])

        def store_planes(g, c):
            words = out_2[g].rearrange("p m t -> p (m t)").bitcast(I32)
            nc.sync.dma_start(words[:, half(c)], planes_c[g, c][:].bitcast(I32))

        def store_plane_scales(g):
            for q in range(4):
                nc.sync.dma_start(out_3[g][4 * q:4 * q + 4, :].bitcast(I32),
                                  planes_s[g][32 * q:32 * q + 4, :].bitcast(I32))

        whole = slice(0, S)
        whole_list = slice(0, S // 16)

        def signal(s):
            for hf in range(2):
                z_matmuls(s, z_bank(s, hf), half(hf))
                z_abs(s, z_bank(s, hf), half(hf))
            for step in (z_exp, gained):
                for hf in range(2):
                    step(s, half(hf))
            scatter(s, whole, whole_list)

        nc.vector.memset(tabs[:].bitcast(I32), 0)
        nc.vector.memset(w4s[:].rearrange("p g n -> p (g n)").bitcast(I32), 0)
        make_identity(nc, ident[:])
        nc.sync.dma_start(idx[:], offs)
        load_table(0)
        nc.sync.dma_start(wgs_rows[:], wgs)
        for q in range(4):
            nc.sync.dma_start(tabs[32 * q:32 * q + 4 * PASSES, :].bitcast(I32),
                              tab_scales[:, 4 * q:4 * q + 4, :].bitcast(I32))
        load_w1(0, 0)
        nc.sync.dma_start(gain_sb[:], gain.rearrange("(g p t) -> p g t", g=GROUPS, t=PACK))
        load_w1(0, 1)
        load_table(1)
        nc.sync.dma_start(idx2[:], offs2)
        load_w1(0, 2)
        nc.sync.dma_start(idx3[:], offs3)
        load_table(2)
        load_page(0)
        load_page(1)

        for hf in range(2):
            turn_wgs(hf)
        nc.vector.tensor_copy(vw[0][:], tabw[0][:].indirect(idx[:]))
        nc.vector.tensor_copy(vs[:], tabs[:].indirect(idx[:]))
        prep_w1(0, 0, 0)
        quantise_w1(0, 0)
        prep_w1(0, 1, 0)
        quantise_w1(0, 1)
        nc.vector.tensor_copy(vw[1][:], tabw[1][:].indirect(idx[:]))
        prep_w1(0, 2, 0)
        quantise_w1(0, 2)
        for picks in FIRST:
            nc.vector.tensor_copy(vw[2][:, picks], tabw[2][:].indirect(idx[:, picks.start // 16:picks.stop // 16]))

        for t in range(PACK):
            for hf in range(2):
                deal_wgs(t, hf)
        for c in range(3):
            quad[c] = tile("quad%d" % c, [P, PACK, HALF], F32)
        load_w1(1, 0)
        load_w1(1, 1)
        load_page(2)
        load_w1(1, 2)
        nc.sync.dma_start(bias_sb[:], bias.rearrange("(g p t) -> p g t", g=GROUPS, t=PACK))
        load_page(3)

        for bank, picks in zip(banks, FIRST):
            z_matmuls(0, bank, picks)
            z_abs(0, bank, picks)
            z_exp(0, picks)
            gained(0, picks)
            scatter(0, picks, slice(picks.start // 16, picks.stop // 16))
        quad[3] = tile("quad3", [P, PACK, HALF], F32, tag="tabw0")
        quad[5] = tile("quad5", [P, PACK, HALF], F32, tag="tabw2")
        planes_g1 = tile("planes_c1", [P, T2], U32, tag="tabw1")
        for c in range(CHUNKS):
            planes_c[1, c] = planes_g1[:, half(c)]
        planes_s[0] = tile("planes_s0", [P, T2], U8, tag="tabs")

        every = range(CHUNKS)
        gather_x(0, whole, whole_list)
        signal(1)
        gather_x(1, whole, whole_list)
        signal(2)
        w1c[1, 0] = tile("w1c10", [P, KP], U32, tag="h1")
        pair = tile("w1c11", [P, 2, KP], U32, tag="h0")
        w1c[1, 1] = pair[:, 0, :]
        w1c[1, 2] = pair[:, 1, :]
        for a in range(PASSES):
            prep_w1(1, a)
            quantise_w1(1, a)
        signal(3)
        xil[0] = tile("xil0", [P, PACK, PX], BF16, tag="raw2")
        xil[1] = tile("xil1", [P, PACK, PX], BF16, tag="raw1")
        nc.sync.dma_start(raw[0][:].rearrange("p (g x) -> p g x", g=GROUPS),
                          w3.rearrange("(g p j) n -> p g (j n)", g=GROUPS, j=PACK))
        regroup(0, every)
        regroup(1, every)
        store_page(0)
        load_page(4)
        regroup(2, every)
        store_page(1)
        regroup(3, every)
        load_page(5)
        store_page(2)
        load_page(6)
        store_page(3)
        load_page(7)
        nc.sync.dma_start(w4c[:].bitcast(I32), w4_words.rearrange("g p b -> p g b").bitcast(I32))
        for q in range(4):
            nc.sync.dma_start(w4s[32 * q:32 * q + 4, :, :].bitcast(I32),
                              w4_scales[:, 4 * q:4 * q + 4, :].rearrange("g r n -> r g n").bitcast(I32))
        round_x(0, whole)
        gather_x(2, whole, whole_list)
        round_x(1, whole)
        gather_x(3, whole, whole_list)
        signal(4)
        late["w3c"] = tile("w3c", [P, GROUPS * N], U32, tag="wgs0")
        prep_w3()
        quantise_w3()
        quad[4] = tile("quad4", [P, PACK, HALF], F32, tag="raw0")
        round_x(2, whole)
        gather_x(4, whole, whole_list)
        signal(5)
        planes_c[0, 0] = tile("planes_c00", [P, HALF], U32, tag="wgs1")
        round_x(3, whole)
        gather_x(5, whole, whole_list)
        weave_x(0, 0, False, stage[3])
        weave_x(0, 1, False, stage[0])
        weave_page(0, 0, False, stage[1])
        quantise_page(0, 0, stage[1])
        signal(6)
        pair = tile("planes_c01", [P, HALF], U32, tag="wgs2")
        planes_c[0, 1] = pair
        pair = tile("xc0", [P, 2, HALF], U32, tag="h2")
        xc[0, 0] = pair[:, 0, :]
        xc[0, 1] = pair[:, 1, :]
        quantise_x(0, 0, stage[3])
        quantise_x(0, 1, stage[0])
        round_x(4, whole)
        gather_x(6, whole, whole_list)
        weave_page(0, 1, False, stage[2])
        quantise_page(0, 1, stage[2])
        weave_page(0, 2, False, stage[4])
        signal(7)
        pair = tile("planes_c02", [P, 2, HALF], U32, tag="wgs3")
        for c in (2, 3):
            planes_c[0, c] = pair[:, c - 2, :]
        round_x(5, whole)
        for hf in range(2):
            gather_x(7, half(hf), list_half(hf))
        round_x(6, whole)
        pair = tile("xc1", [P, 2, HALF], U32, tag="h0")
        for hf in range(2):
            xc[1, hf] = pair[:, hf, :]
            weave_x_early(hf, stage[5 + hf])
        weave_page(0, 3, False, stage[1])
        for hf in range(2):
            last_x(hf, stage[5 + hf])
        quantise_page(0, 2, stage[4])
        quantise_page(0, 3, stage[1])
        regroup(4, (0, 1))
        store_page(4)
        regroup(5, (0, 1))
        regroup(4, (2,))
        regroup(5, (2,))
        store_planes(0, 0)
        store_page(5)
        regroup(6, (0, 1, 2))
        for s in (4, 5, 6):
            regroup(s, (3,))
        store_planes(0, 1)
        store_page(6)
        regroup(7, (0, 2, 3))
        store_page(7)
        regroup(7, (1,))
        for g in range(GROUPS):
            y_matmuls(g, 0)
        for g in range(GROUPS):
            y_matmuls(g, 1)
        store_planes(0, 2)
        store_planes(0, 3)
        store_plane_scales(0)
        for c, st in ((0, 3), (1, 0), (2, 2), (3, 4)):
            weave_page(1, c, c >= 2, stage[st])
            quantise_page(1, c, stage[st])
        for c in (0, 2, 3):
            store_planes(1, c)
        late["y", 0] = tile("y0", [P, PX], F32, tag="raw0")
        late["y", 1] = tile("y1", [P, PX], F32, tag="tabw2")
        y_out(0)
        store_planes(1, 1)
        store_plane_scales(1)
        y_out(1)
